import numpy as np
import ml_dtypes


def mxq(x, axis, fmt="e4m3"):
    dtype, down = {"e4m3": (ml_dtypes.float8_e4m3fn, 7), "e5m2": (ml_dtypes.float8_e5m2, 14)}[fmt]
    v = np.moveaxis(np.asarray(x, np.float32).astype(ml_dtypes.bfloat16).astype(np.float64), axis, -1)
    blocks = v.reshape(v.shape[:-1] + (-1, 32))
    amax = np.abs(blocks).max(-1, keepdims=True)
    byte = np.maximum(np.where(amax > 0, np.frexp(amax)[1] - 1 + 127, 0) - down, 1)
    scale = np.exp2(byte - 127.0)
    codes = (blocks / scale).astype(np.float32).astype(dtype).astype(np.float64)
    return np.moveaxis((codes * scale).reshape(v.shape), -1, axis)


WIDE = False


def mx_kscale(k):
    if not WIDE:
        return np.ones(k)
    levels = np.array([10, -10, 5, -5, 0])
    if k % 512:
        return np.exp2(np.random.permutation(np.resize(levels, k // 32))).repeat(32)
    a = np.empty((k // 512, 16))
    for p in range(k // 512):
        a[p, :8] = np.random.permutation(np.resize(levels, 8))
        for g in range(8):
            far = levels[np.abs(levels - a[p, g]) >= 10]
            a[p, g + 8] = far[np.random.randint(len(far))]
    return np.exp2(a.ravel()).repeat(32)


def f64(x):
    return np.asarray(x).astype(np.float64)


def striped(idx):
    return np.tile(idx.reshape(-1, 16).T, (8, 1)).astype(np.uint16)


def unstriped(offs):
    return offs[:16].T.reshape(-1).astype(np.int64)


E2M1 = np.array([0.0, 0.5, 1.0, 1.5, 2.0, 3.0, 4.0, 6.0, -0.0, -0.5, -1.0, -1.5, -2.0, -3.0, -4.0, -6.0])


def pack_weight(w, fmt):
    k, n = w.shape
    w = f64(np.asarray(w, np.float32).astype(ml_dtypes.bfloat16)).reshape(k // 32, 32, n)
    amax = np.abs(w).max(1)
    if fmt == "e4m3":
        byte = np.frexp(amax)[1] - 1 + 127 - 7
    else:
        mant, ex = np.frexp(amax / 6.0)
        byte = np.where(mant > 0.5, ex, ex - 1) + 127
    byte = np.clip(np.where(amax > 0, byte, 1), 1, 254)
    scaled = (w * np.exp2(127.0 - byte)[:, None, :]).reshape(k, n).astype(np.float32)
    by_word = np.ascontiguousarray(scaled.reshape(k // 512, 128, 4, n).transpose(0, 1, 3, 2))
    if fmt == "e4m3":
        words = by_word.astype(ml_dtypes.float8_e4m3fn).view(np.uint8)
    else:
        c = by_word.astype(ml_dtypes.float4_e2m1fn).view(np.uint8) & 0xF
        words = (c[..., 0::2] | (c[..., 1::2] << 4)).reshape(k // 512, 128, 2 * n)
    return np.ascontiguousarray(words), np.ascontiguousarray(byte.astype(np.uint8).reshape(k // 512, 16, n))


def unpack_weight(words, scales, fmt):
    g, _, n = scales.shape
    words = np.ascontiguousarray(words).reshape(g, 128, n, -1)
    if fmt == "e4m3":
        vals = words.view(ml_dtypes.float8_e4m3fn).astype(np.float64)
    else:
        nib = np.empty((g, 128, n, 4), np.uint8)
        nib[..., 0::2] = words & 0xF
        nib[..., 1::2] = words >> 4
        vals = E2M1[nib]
    vals = vals * np.repeat(np.exp2(scales.astype(np.float64) - 127.0), 8, axis=1)[..., None]
    return vals.transpose(0, 1, 3, 2).reshape(g * 512, n)


def gelu(v):
    return 0.5 * v * (1.0 + np.tanh(np.sqrt(2.0 / np.pi) * (v + 0.044715 * v**3)))


K, M, H, N, T, S, P, T2 = 1024, 512, 1024, 512, 2048, 1024, 512, 2048


def setup_inputs():
    n = np.random.standard_normal
    s, s2, u = mx_kscale(K)[:, None], mx_kscale(M)[:, None], mx_kscale(H)[:, None]
    tab_words, tab_scales = pack_weight(n((K, T)) * s, "e4m3")
    tab2_words, tab2_scales = pack_weight(n((M, T)) * s2, "e4m3")
    w2_words, w2_scales = pack_weight(0.45 * n((M, H)) / s2 / np.sqrt(M), "e2m1")
    w4_words, w4_scales = pack_weight(1.3 * n((H, N)) / u / np.sqrt(H), "e4m3")
    perm = np.random.permutation(T2)
    return {
        "tab_words": tab_words, "tab_scales": tab_scales,
        "tab2_words": tab2_words, "tab2_scales": tab2_scales,
        "offs": striped(np.random.permutation(T)[:S]),
        "offs2": striped(np.random.permutation(T)[:P]),
        "pos1": striped(np.random.permutation(S)[:P]),
        "offs3": striped(perm[:S]), "offs4": striped(perm[S:S + P]),
        "w1": (1.1 * n((K, H)) / s * u.T / np.sqrt(K)).astype(np.float32),
        "w2_words": w2_words, "w2_scales": w2_scales,
        "beta": (np.random.uniform(0.5, 2.5, H) / u[:, 0]).astype(np.float32),
        "phase": np.random.uniform(-0.9, 0.9, H).astype(np.float32),
        "w3": (1.4 * n((H, N)) / u / np.sqrt(H)).astype(np.float32),
        "w4_words": w4_words, "w4_scales": w4_scales,
        "wg1": np.exp(0.3 * n((128, S))).astype(np.float32),
        "wg2": np.exp(0.3 * n((128, P))).astype(np.float32),
        "page1": n((N, T2)).astype(np.float32),
    }


def reference(tab_words, tab_scales, tab2_words, tab2_scales, offs, offs2, pos1, offs3, offs4, w1, w2_words, w2_scales,
              beta, phase, w3, w4_words, w4_scales, wg1, wg2, page1):
    v = unpack_weight(tab_words, tab_scales, "e4m3")[:, unstriped(offs)]
    v2 = unpack_weight(tab2_words, tab2_scales, "e4m3")[:, unstriped(offs2)]
    h1 = mxq(f64(w1), 0, "e4m3").T @ v
    h2 = unpack_weight(w2_words, w2_scales, "e2m1").T @ v2
    x = h1 * f64(beta)[:, None]
    z1 = 0.5 * h1 * (1.0 + np.tanh(0.7978845608 * (x + 0.044715 * x ** 3)))
    z2 = np.cos(h2 + f64(phase)[:, None]) * h1[:, unstriped(pos1)]
    y1 = mxq(f64(w3), 0, "e4m3").T @ mxq(z1, 0, "e4m3")
    y2 = unpack_weight(w4_words, w4_scales, "e4m3").T @ mxq(z2, 0, "e4m3")
    out = f64(page1).copy()
    out[:, unstriped(offs3)] = np.tile(f64(wg1), (N // 128, 1)) * y1
    out[:, unstriped(offs4)] = np.tile(f64(wg2), (N // 128, 1)) * y2
    return out

@@ -1,0 +1,309 @@
+import math
+from contextlib import ExitStack
+
+import concourse.mybir as mybir
+
+K, M, H, N, T, S, PK, T2 = 1024, 512, 1024, 512, 2048, 1024, 512, 2048
+FLOPS = 2 * (K * H * S + M * H * PK + H * N * S + H * N * PK)
+
+F32 = mybir.dt.float32
+BF16 = mybir.dt.bfloat16
+I32 = mybir.dt.int32
+U32 = mybir.dt.uint32
+U16 = mybir.dt.uint16
+U8 = mybir.dt.uint8
+FP8X4 = mybir.dt.float8_e4m3fn_x4
+FP4X4 = mybir.dt.float4_e2m1fn_x4
+ACT = mybir.ActivationFunctionType
+ALU = mybir.AluOpType
+
+P = 128
+W = 512
+TWO_PI = 2.0 * math.pi
+
+W1_ON_VECTOR = ((1, 1),)
+W3_ON_VECTOR = ()
+Z1_ON_VECTOR = ((0, 1),)
+CHUNKS = ((0, 512), (512, 512))
+
+
+def tile_list_repayment_feature_page_kernel(
+    tc, tab_words, tab_scales, tab2_words, tab2_scales, offs, offs2, pos1, offs3, offs4, w1, w2_words, w2_scales,
+    beta, phase, w3, w4_words, w4_scales, wg1, wg2, page1, out,
+):
+    nc = tc.nc
+    with ExitStack() as ctx:
+        lists = ctx.enter_context(tc.tile_pool(name="lists", bufs=1))
+        keep = ctx.enter_context(tc.tile_pool(name="keep", bufs=1))
+        slots = ctx.enter_context(tc.tile_pool(name="slots", bufs=1))
+        ring = ctx.enter_context(tc.tile_pool(name="ring", bufs=4))
+        psum = ctx.enter_context(tc.psum_pool(name="psum", bufs=8))
+
+        def held(name, shape, dtype):
+            return keep.tile(shape, dtype, name=name, align_bytes=64)
+
+        def slot(tag, name, shape, dtype):
+            return slots.tile(shape, dtype, name=name, tag=tag, align_bytes=64)
+
+        def load_list(name, src):
+            tl = lists.tile(list(src.shape), U16, name=name)
+            nc.sync.dma_start(tl[:], src)
+            return tl
+
+        def zeroed_plane(name, width):
+            plane = held(name, [P, width], U8)
+            nc.vector.memset(plane[:].bitcast(I32), 0)
+            return plane
+
+        def load_plane(queue, plane, src):
+            passes = src.shape[0]
+            for q in range(4):
+                queue.dma_start(out=plane[32 * q : 32 * q + 4 * passes, :].bitcast(I32),
+                                in_=src[:, 4 * q : 4 * q + 4, :].bitcast(I32))
+
+        def load_words(tl, src):
+            nc.sync.dma_start(out=tl[:], in_=src.rearrange("p n i -> p (n i)").bitcast(I32))
+
+        def load_rows(tl, src):
+            nc.sync.dma_start(out=tl[:], in_=src.rearrange("(p i) c -> p i c", i=4))
+
+        def bank():
+            return psum.tile([P, W], F32, name="bank")
+
+        def cast(on_vector, dst, src):
+            if on_vector:
+                nc.vector.tensor_copy(out=dst, in_=src)
+            else:
+                nc.scalar.copy(out=dst, in_=src)
+
+        def quantise(name, grouped, width=W):
+            codes = held(name + "_codes", [P, width], U32)
+            scales = held(name + "_scales", [P, width], U8)
+            nc.vector.quantize_mx(out=codes[:].bitcast(FP8X4), scales=scales[:], in_=grouped[:])
+            return codes, scales
+
+        def staged(width=W):
+            return ring.tile([P, 4 * width], BF16, name="grouped", align_bytes=64)
+
+        def woven(tl):
+            return tl[:].rearrange("p (c e t) -> p c t e", e=4, t=4)
+
+        def by_rows(tl):
+            return tl[:].rearrange("p t (c e) -> p c t e", e=4)
+
+        tab2_plane = zeroed_plane("tab2_plane", T)
+        w2_plane = zeroed_plane("w2_plane", H)
+        tab_plane = zeroed_plane("tab_plane", T)
+        w4_plane = zeroed_plane("w4_plane", N)
+
+        w1_raw = {}
+
+        def load_w1(a, b, tag):
+            w1_raw[a, b] = slot(tag, "w1_raw%d%d" % (a, b), [P, 4, W], F32)
+            load_rows(w1_raw[a, b], w1[W * a : W * (a + 1), W * b : W * (b + 1)])
+
+        w2_raw = held("w2_raw", [P, H // 2], I32)
+        nc.sync.dma_start(out=w2_raw[:], in_=w2_words[0].bitcast(I32))
+        idx2 = load_list("idx2", offs2)
+        tab2_sb = slot("A", "tab2_sb", [P, T], I32)
+        load_words(tab2_sb, tab2_words[0])
+        load_plane(nc.sync, w2_plane, w2_scales)
+        load_plane(nc.sync, tab2_plane, tab2_scales)
+        load_w1(0, 0, "B")
+        phase_sb = held("phase_sb", [P, 2, 4], F32)
+        nc.sync.dma_start(out=phase_sb[:], in_=phase.rearrange("(b p t) -> p b t", p=P, t=4))
+        idx = load_list("idx", offs)
+        load_plane(nc.sync, tab_plane, tab_scales)
+        tab_sb = [slot("D", "tab_sb0", [P, T], I32), slot("E", "tab_sb1", [P, T], I32)]
+        load_words(tab_sb[0], tab_words[0])
+        load_w1(1, 0, "C")
+        load_words(tab_sb[1], tab_words[1])
+        load_w1(0, 1, "F")
+        load_w1(1, 1, "G")
+        idx_p = load_list("idx_p", pos1)
+        beta_sb = held("beta_sb", [P, 2, 4], F32)
+        nc.sync.dma_start(out=beta_sb[:], in_=beta.rearrange("(b p t) -> p b t", p=P, t=4))
+
+        w1_q = {}
+
+        def round_w1(a, b):
+            grouped = staged()
+            cast((a, b) in W1_ON_VECTOR, grouped[:].rearrange("p (t m i) -> p m i t", t=4, i=4),
+                 w1_raw[a, b][:].rearrange("p i (m t) -> p m i t", t=4))
+            return grouped
+
+        def quantise_w1(a, b, grouped):
+            w1_q[a, b] = quantise("w1_%d%d" % (a, b), grouped)
+
+        v_codes = [held("v_codes0", [P, S], U32), held("v_codes1", [P, S], U32)]
+        v_scales = held("v_scales", [P, S], U8)
+        w2_dealt = held("w2_dealt", [P, H], U16)
+        nc.vector.tensor_copy(out=w2_dealt[:].rearrange("p (b t m) -> p b m t", b=2, t=4),
+                              in_=w2_raw[:].bitcast(U16).rearrange("p (b m t) -> p b m t", b=2, t=4))
+        v2_codes = held("v2_codes", [P, PK], U32)
+        nc.vector.tensor_copy(v2_codes[:], tab2_sb[:].bitcast(U32).indirect(idx2[:]))
+        w2_plane_dealt = held("w2_plane_dealt", [P, H], U8)
+        nc.vector.tensor_copy(out=w2_plane_dealt[:].rearrange("p (b t m) -> p b m t", b=2, t=4),
+                              in_=w2_plane[:].rearrange("p (b m t) -> p b m t", b=2, t=4))
+        v2_scales = held("v2_scales", [P, PK], U8)
+        nc.vector.tensor_copy(v2_scales[:], tab2_plane[:].indirect(idx2[:]))
+        turns0 = held("turns0", [P, 8], F32)
+        nc.vector.tensor_scalar(out=turns0[:], in0=phase_sb[:].rearrange("p b t -> p (b t)"), scalar1=1.0 / TWO_PI,
+                                scalar2=None, op0=ALU.mult)
+
+        h1 = {}
+        picked = [None, None]
+
+        def first_stage(b):
+            for t in range(4):
+                h1[b, t] = held("h1_%d%d" % (b, t), [P, S], F32)
+                for jh in range(2):
+                    cols = slice(W * jh, W * (jh + 1))
+                    acc = bank()
+                    for a in range(2):
+                        codes, scales = w1_q[a, b]
+                        nc.tensor.matmul_mx(out=acc[:], lhsT=codes[:, P * t : P * (t + 1)].bitcast(FP8X4),
+                                            lhsT_scale=scales[:, P * t : P * (t + 1)],
+                                            rhs=v_codes[a][:, cols].bitcast(FP8X4), rhs_scale=v_scales[4 * a : P, cols],
+                                            start=(a == 0), stop=(a == 1))
+                    nc.scalar.copy(out=h1[b, t][:, cols], in_=acc[:])
+
+        def pick(b):
+            picked[b] = slot("CD"[b], "picked%d" % b, [P, 4, PK], F32)
+            for t in range(4):
+                nc.vector.tensor_copy(picked[b][:, t, :], h1[b, t][:].indirect(idx_p[:]))
+
+        turns = [slot("H", "turns_b0", [P, 4, PK], F32), slot("I", "turns_b1", [P, 4, PK], F32)]
+        whole = [slot("J", "whole_b0", [P, 4, PK], I32), slot("K", "whole_b1", [P, 4, PK], I32)]
+
+        def angles(b):
+            for t in range(4):
+                s = 4 * b + t
+                acc = bank()
+                nc.tensor.matmul_mx(out=acc[:], lhsT=w2_dealt[:, P * s : P * (s + 1)].bitcast(FP4X4),
+                                    lhsT_scale=w2_plane_dealt[:, P * s : P * (s + 1)],
+                                    rhs=v2_codes[:].bitcast(FP8X4), rhs_scale=v2_scales[:], start=True, stop=True)
+                nc.scalar.activation(out=turns[b][:, t, :], in_=acc[:], func=ACT.Abs,
+                                     bias=turns0[:, s : s + 1], scale=1.0 / TWO_PI)
+
+        def reduce_turns(b):
+            nc.vector.tensor_scalar(out=whole[b][:], in0=turns[b][:], scalar1=0.25, scalar2=None, op0=ALU.add)
+            nc.vector.scalar_tensor_tensor(out=turns[b][:], in0=turns[b][:], scalar=0.25, in1=whole[b][:],
+                                           op0=ALU.add, op1=ALU.subtract)
+
+        def cosine(b):
+            nc.scalar.activation(out=turns[b][:], in_=turns[b][:], func=ACT.Sin, scale=TWO_PI)
+
+        def make_z2(b):
+            grouped = staged()
+            nc.vector.tensor_tensor(out=woven(grouped), in0=by_rows(picked[b]), in1=by_rows(turns[b]), op=ALU.mult)
+            return grouped
+
+        w1_00 = round_w1(0, 0)
+        angles(0)
+        nc.vector.tensor_copy(v_scales[:], tab_plane[:].indirect(idx[:]))
+        quantise_w1(0, 0, w1_00)
+        nc.vector.tensor_copy(v_codes[0][:], tab_sb[0][:].bitcast(U32).indirect(idx[:]))
+        w1_10 = round_w1(1, 0)
+        angles(1)
+        nc.vector.tensor_copy(v_codes[1][:], tab_sb[1][:].bitcast(U32).indirect(idx[:]))
+        quantise_w1(1, 0, w1_10)
+        reduce_turns(0)
+        w1_01 = round_w1(0, 1)
+        first_stage(0)
+        quantise_w1(0, 1, w1_01)
+        w1_11 = round_w1(1, 1)
+        reduce_turns(1)
+        quantise_w1(1, 1, w1_11)
+        pick(0)
+        cosine(0)
+        first_stage(1)
+        cosine(1)
+
+        w3_raw = [slot("A", "w3_raw0", [P, 4, W], F32), slot("B", "w3_raw1", [P, 4, W], F32)]
+        w4_sb = held("w4_sb", [P, 2, N], I32)
+        nc.sync.dma_start(out=w4_sb[:], in_=w4_words.rearrange("a p n i -> p a (n i)").bitcast(I32))
+        load_plane(nc.sync, w4_plane, w4_scales)
+        load_rows(w3_raw[0], w3[0:W, :])
+        load_rows(w3_raw[1], w3[W : 2 * W, :])
+        idx4 = load_list("idx4", offs4)
+        idx3 = load_list("idx3", offs3)
+        wg2_sb = held("wg2_sb", [P, PK], F32)
+        nc.sync.dma_start(out=wg2_sb[:], in_=wg2)
+        page = [held("page0", [P, T2], F32), held("page1", [P, T2], F32),
+                slot("E", "page2", [P, T2], F32), slot("F", "page3", [P, T2], F32)]
+        for q in range(4):
+            nc.sync.dma_start(out=page[q][:], in_=page1[P * q : P * (q + 1), :])
+        wg1_sb = held("wg1_sb", [P, S], F32)
+        nc.sync.dma_start(out=wg1_sb[:], in_=wg1)
+
+        inv_beta = held("inv_beta", [P, 8], F32)
+        nc.vector.reciprocal(out=inv_beta[:], in_=beta_sb[:].rearrange("p b t -> p (b t)"))
+
+        def second_stage(q, weights, acts, width, late=False):
+            acc = bank()
+            for b in range(2):
+                w_codes, w_scales = weights[b]
+                z_codes, z_scales = acts[b]
+                nc.tensor.matmul_mx(out=acc[:, 0:width], lhsT=w_codes[:, P * q : P * (q + 1)].bitcast(FP8X4),
+                                    lhsT_scale=w_scales[:, P * q : P * (q + 1)],
+                                    rhs=z_codes[:, 0:width].bitcast(FP8X4), rhs_scale=z_scales[:, 0:width],
+                                    start=(b == 0), stop=(b == 1))
+            y = slot("K", "y_late", [P, W], F32) if late else keep.tile([P, W], F32, name="y", tag="y", bufs=4)
+            nc.scalar.copy(out=y[:, 0:width], in_=acc[:, 0:width])
+            return y
+
+        def gelu_rows(c, b):
+            j0, width = CHUNKS[c]
+            g = slot("JK"[b], "g%d%d" % (c, b), [P, 4, width], F32)
+            for t in range(4):
+                nc.scalar.activation(out=g[:, t, :], in_=h1[b, t][:, j0 : j0 + width], func=ACT.Gelu_apprx_tanh,
+                                     scale=beta_sb[:, b, t : t + 1])
+            return g
+
+        def make_z1(c, b, g):
+            width = CHUNKS[c][1]
+            grouped = staged(width)
+            if (c, b) in Z1_ON_VECTOR:
+                factor = inv_beta[:, 4 * b : 4 * b + 4].unsqueeze(1).unsqueeze(3).to_broadcast([P, width // 4, 4, 4])
+                nc.vector.tensor_tensor(out=woven(grouped), in0=by_rows(g), in1=factor, op=ALU.mult)
+            else:
+                rows = keep.tile([P, 4, width], BF16, name="z1_rows", tag="z1_rows")
+                for t in range(4):
+                    nc.scalar.activation(out=rows[:, t, :], in_=g[:, t, :], func=ACT.Copy,
+                                         scale=inv_beta[:, 4 * b + t : 4 * b + t + 1])
+                nc.scalar.copy(out=woven(grouped), in_=by_rows(rows))
+            return grouped
+
+        def round_w3(b):
+            grouped = staged()
+            cast(b in W3_ON_VECTOR, woven(grouped), by_rows(w3_raw[b]))
+            return grouped
+
+        w4_q = [(w4_sb[:, b, :].bitcast(U32), w4_plane[4 * b : P, :]) for b in range(2)]
+        z2_0 = make_z2(0)
+        pick(1)
+        w3_0 = round_w3(0)
+        z2_q = [quantise("z2_0", z2_0)]
+        z2_1 = make_z2(1)
+        w3_q = [quantise("w3_0", w3_0)]
+        z2_q.append(quantise("z2_1", z2_1))
+        w3_1 = round_w3(1)
+        w3_q.append(quantise("w3_1", w3_1))
+        stages = [(w4_q, PK, idx4[:], wg2_sb[:])]
+        stages.extend((w3_q, width, idx3[:, j0 // 16 : (j0 + width) // 16], wg1_sb[:, j0 : j0 + width]) for j0, width in CHUNKS)
+        acts = z2_q
+        for c, (weights, width, where, factor_sb) in enumerate(stages):
+            last = c == len(CHUNKS)
+            early = 4 if last else 3
+            y_tiles = [second_stage(q, weights, acts, width) for q in range(early)]
+            z1_q = []
+            for q in range(4):
+                if q == early:
+                    for b in range(2):
+                        z1_q.append(quantise("z1_%d%d" % (c, b), make_z1(c, b, gelu_rows(c, b)), CHUNKS[c][1]))
+                    y_tiles.append(second_stage(q, weights, acts, width, late=True))
+                nc.vector.tensor_tensor(page[q][:].indirect(where), y_tiles[q][:, 0:width], factor_sb, ALU.mult)
+                if last:
+                    nc.sync.dma_start(out=out[P * q : P * (q + 1), :], in_=page[q][:])
+            acts = z1_q

@@ -21,9 +21,14 @@ P = 128
 W = 512
 TWO_PI = 2.0 * math.pi
 
-W1_ON_VECTOR = ((1, 1),)
-W3_ON_VECTOR = ()
-Z1_ON_VECTOR = ((0, 1),)
+W1_ENGINE = ("scalar", "scalar", "vector", "vector")
+W3_ENGINE = ("scalar", "scalar")
+Z2_ENGINE = ("vector", "vector")
+Z1_HOW = "VSSS"
+WHOLE_ON_SCALAR = ()
+PRE = (1, 2)
+GSLOT = "JKGH"
+FUSED = True
 CHUNKS = ((0, 512), (512, 512))
 
 
@@ -70,9 +75,11 @@ def tile_list_repayment_feature_page_kernel(
         def bank():
             return psum.tile([P, W], F32, name="bank")
 
-        def cast(on_vector, dst, src):
-            if on_vector:
+        def cast(engine, dst, src):
+            if engine == "vector":
                 nc.vector.tensor_copy(out=dst, in_=src)
+            elif engine == "gpsimd":
+                nc.gpsimd.tensor_scalar(out=dst, in0=src, scalar1=1.0, scalar2=0.0, op0=ALU.mult, op1=ALU.add)
             else:
                 nc.scalar.copy(out=dst, in_=src)
 
@@ -91,9 +98,9 @@ def tile_list_repayment_feature_page_kernel(
         def by_rows(tl):
             return tl[:].rearrange("p t (c e) -> p c t e", e=4)
 
-        tab2_plane = zeroed_plane("tab2_plane", T)
-        w2_plane = zeroed_plane("w2_plane", H)
         tab_plane = zeroed_plane("tab_plane", T)
+        w2_plane = zeroed_plane("w2_plane", H)
+        tab2_plane = zeroed_plane("tab2_plane", T)
         w4_plane = zeroed_plane("w4_plane", N)
 
         w1_raw = {}
@@ -103,18 +110,18 @@ def tile_list_repayment_feature_page_kernel(
             load_rows(w1_raw[a, b], w1[W * a : W * (a + 1), W * b : W * (b + 1)])
 
         w2_raw = held("w2_raw", [P, H // 2], I32)
-        nc.sync.dma_start(out=w2_raw[:], in_=w2_words[0].bitcast(I32))
-        idx2 = load_list("idx2", offs2)
         tab2_sb = slot("A", "tab2_sb", [P, T], I32)
-        load_words(tab2_sb, tab2_words[0])
-        load_plane(nc.sync, w2_plane, w2_scales)
-        load_plane(nc.sync, tab2_plane, tab2_scales)
-        load_w1(0, 0, "B")
         phase_sb = held("phase_sb", [P, 2, 4], F32)
-        nc.sync.dma_start(out=phase_sb[:], in_=phase.rearrange("(b p t) -> p b t", p=P, t=4))
+        tab_sb = [slot("D", "tab_sb0", [P, T], I32), slot("E", "tab_sb1", [P, T], I32)]
+        nc.sync.dma_start(out=w2_raw[:], in_=w2_words[0].bitcast(I32))
         idx = load_list("idx", offs)
         load_plane(nc.sync, tab_plane, tab_scales)
-        tab_sb = [slot("D", "tab_sb0", [P, T], I32), slot("E", "tab_sb1", [P, T], I32)]
+        idx2 = load_list("idx2", offs2)
+        load_words(tab2_sb, tab2_words[0])
+        load_w1(0, 0, "B")
+        load_plane(nc.sync, w2_plane, w2_scales)
+        load_plane(nc.sync, tab2_plane, tab2_scales)
+        nc.sync.dma_start(out=phase_sb[:], in_=phase.rearrange("(b p t) -> p b t", p=P, t=4))
         load_words(tab_sb[0], tab_words[0])
         load_w1(1, 0, "C")
         load_words(tab_sb[1], tab_words[1])
@@ -128,7 +135,7 @@ def tile_list_repayment_feature_page_kernel(
 
         def round_w1(a, b):
             grouped = staged()
-            cast((a, b) in W1_ON_VECTOR, grouped[:].rearrange("p (t m i) -> p m i t", t=4, i=4),
+            cast(W1_ENGINE[2 * b + a], grouped[:].rearrange("p (t m i) -> p m i t", t=4, i=4),
                  w1_raw[a, b][:].rearrange("p i (m t) -> p m i t", t=4))
             return grouped
 
@@ -137,6 +144,7 @@ def tile_list_repayment_feature_page_kernel(
 
         v_codes = [held("v_codes0", [P, S], U32), held("v_codes1", [P, S], U32)]
         v_scales = held("v_scales", [P, S], U8)
+        nc.vector.tensor_copy(v_scales[:], tab_plane[:].indirect(idx[:]))
         w2_dealt = held("w2_dealt", [P, H], U16)
         nc.vector.tensor_copy(out=w2_dealt[:].rearrange("p (b t m) -> p b m t", b=2, t=4),
                               in_=w2_raw[:].bitcast(U16).rearrange("p (b m t) -> p b m t", b=2, t=4))
@@ -171,7 +179,7 @@ def tile_list_repayment_feature_page_kernel(
         def pick(b):
             picked[b] = slot("CD"[b], "picked%d" % b, [P, 4, PK], F32)
             for t in range(4):
-                nc.vector.tensor_copy(picked[b][:, t, :], h1[b, t][:].indirect(idx_p[:]))
+                nc.vector.tensor_tensor(picked[b][:, t, :], h1[b, t][:].indirect(idx_p[:]), turns[b][:, t, :], ALU.mult)
 
         turns = [slot("H", "turns_b0", [P, 4, PK], F32), slot("I", "turns_b1", [P, 4, PK], F32)]
         whole = [slot("J", "whole_b0", [P, 4, PK], I32), slot("K", "whole_b1", [P, 4, PK], I32)]
@@ -187,7 +195,10 @@ def tile_list_repayment_feature_page_kernel(
                                      bias=turns0[:, s : s + 1], scale=1.0 / TWO_PI)
 
         def reduce_turns(b):
-            nc.vector.tensor_scalar(out=whole[b][:], in0=turns[b][:], scalar1=0.25, scalar2=None, op0=ALU.add)
+            if b in WHOLE_ON_SCALAR:
+                nc.scalar.activation(out=whole[b][:].bitcast(U32), in_=turns[b][:], func=ACT.Copy, bias=0.25, scale=1.0)
+            else:
+                nc.vector.tensor_scalar(out=whole[b][:], in0=turns[b][:], scalar1=0.25, scalar2=None, op0=ALU.add)
             nc.vector.scalar_tensor_tensor(out=turns[b][:], in0=turns[b][:], scalar=0.25, in1=whole[b][:],
                                            op0=ALU.add, op1=ALU.subtract)
 
@@ -196,30 +207,28 @@ def tile_list_repayment_feature_page_kernel(
 
         def make_z2(b):
             grouped = staged()
-            nc.vector.tensor_tensor(out=woven(grouped), in0=by_rows(picked[b]), in1=by_rows(turns[b]), op=ALU.mult)
+            cast(Z2_ENGINE[b], woven(grouped), by_rows(picked[b]))
             return grouped
 
-        w1_00 = round_w1(0, 0)
-        angles(0)
-        nc.vector.tensor_copy(v_scales[:], tab_plane[:].indirect(idx[:]))
-        quantise_w1(0, 0, w1_00)
         nc.vector.tensor_copy(v_codes[0][:], tab_sb[0][:].bitcast(U32).indirect(idx[:]))
-        w1_10 = round_w1(1, 0)
-        angles(1)
+        angles(0)
+        w1_00 = round_w1(0, 0)
         nc.vector.tensor_copy(v_codes[1][:], tab_sb[1][:].bitcast(U32).indirect(idx[:]))
+        w1_10 = round_w1(1, 0)
+        quantise_w1(0, 0, w1_00)
         quantise_w1(1, 0, w1_10)
+        angles(1)
         reduce_turns(0)
-        w1_01 = round_w1(0, 1)
+        cosine(0)
         first_stage(0)
+        w1_01 = round_w1(0, 1)
         quantise_w1(0, 1, w1_01)
         w1_11 = round_w1(1, 1)
-        reduce_turns(1)
         quantise_w1(1, 1, w1_11)
+        reduce_turns(1)
         pick(0)
-        cosine(0)
-        first_stage(1)
         cosine(1)
-
+        first_stage(1)
         w3_raw = [slot("A", "w3_raw0", [P, 4, W], F32), slot("B", "w3_raw1", [P, 4, W], F32)]
         w4_sb = held("w4_sb", [P, 2, N], I32)
         nc.sync.dma_start(out=w4_sb[:], in_=w4_words.rearrange("a p n i -> p a (n i)").bitcast(I32))
@@ -240,7 +249,7 @@ def tile_list_repayment_feature_page_kernel(
         inv_beta = held("inv_beta", [P, 8], F32)
         nc.vector.reciprocal(out=inv_beta[:], in_=beta_sb[:].rearrange("p b t -> p (b t)"))
 
-        def second_stage(q, weights, acts, width, late=False):
+        def second_stage(q, weights, acts, width, late=""):
             acc = bank()
             for b in range(2):
                 w_codes, w_scales = weights[b]
@@ -249,13 +258,18 @@ def tile_list_repayment_feature_page_kernel(
                                     lhsT_scale=w_scales[:, P * q : P * (q + 1)],
                                     rhs=z_codes[:, 0:width].bitcast(FP8X4), rhs_scale=z_scales[:, 0:width],
                                     start=(b == 0), stop=(b == 1))
-            y = slot("K", "y_late", [P, W], F32) if late else keep.tile([P, W], F32, name="y", tag="y", bufs=4)
+            y = slot(late, "y_late", [P, W], F32) if late else keep.tile([P, W], F32, name="y", tag="y", bufs=4)
             nc.scalar.copy(out=y[:, 0:width], in_=acc[:, 0:width])
+            return y
+
+        def weighted(y, factor_sb):
+            if not FUSED:
+                nc.gpsimd.tensor_tensor(out=y[:], in0=y[:], in1=factor_sb, op=ALU.mult)
             return y
 
         def gelu_rows(c, b):
             j0, width = CHUNKS[c]
-            g = slot("JK"[b], "g%d%d" % (c, b), [P, 4, width], F32)
+            g = slot(GSLOT[2 * c + b], "g%d%d" % (c, b), [P, 4, width], F32)
             for t in range(4):
                 nc.scalar.activation(out=g[:, t, :], in_=h1[b, t][:, j0 : j0 + width], func=ACT.Gelu_apprx_tanh,
                                      scale=beta_sb[:, b, t : t + 1])
@@ -264,20 +278,22 @@ def tile_list_repayment_feature_page_kernel(
         def make_z1(c, b, g):
             width = CHUNKS[c][1]
             grouped = staged(width)
-            if (c, b) in Z1_ON_VECTOR:
+            how = Z1_HOW[2 * c + b]
+            if how in "VG":
                 factor = inv_beta[:, 4 * b : 4 * b + 4].unsqueeze(1).unsqueeze(3).to_broadcast([P, width // 4, 4, 4])
-                nc.vector.tensor_tensor(out=woven(grouped), in0=by_rows(g), in1=factor, op=ALU.mult)
+                engine = nc.vector if how == "V" else nc.gpsimd
+                engine.tensor_tensor(out=woven(grouped), in0=by_rows(g), in1=factor, op=ALU.mult)
             else:
-                rows = keep.tile([P, 4, width], BF16, name="z1_rows", tag="z1_rows")
+                rows = keep.tile([P, 4, width], BF16, name="z1_rows", tag="z1_rows", bufs=2)
                 for t in range(4):
                     nc.scalar.activation(out=rows[:, t, :], in_=g[:, t, :], func=ACT.Copy,
                                          scale=inv_beta[:, 4 * b + t : 4 * b + t + 1])
-                nc.scalar.copy(out=woven(grouped), in_=by_rows(rows))
+                cast("scalar" if how == "S" else "gpsimd", woven(grouped), by_rows(rows))
             return grouped
 
         def round_w3(b):
             grouped = staged()
-            cast(b in W3_ON_VECTOR, woven(grouped), by_rows(w3_raw[b]))
+            cast(W3_ENGINE[b], woven(grouped), by_rows(w3_raw[b]))
             return grouped
 
         w4_q = [(w4_sb[:, b, :].bitcast(U32), w4_plane[4 * b : P, :]) for b in range(2)]
@@ -296,14 +312,28 @@ def tile_list_repayment_feature_page_kernel(
         for c, (weights, width, where, factor_sb) in enumerate(stages):
             last = c == len(CHUNKS)
             early = 4 if last else 3
-            y_tiles = [second_stage(q, weights, acts, width) for q in range(early)]
+            gelus, woven_z1 = {}, {}
+            if not last and PRE[c] >= 1:
+                gelus[0] = gelu_rows(c, 0)
+            if not last and PRE[c] >= 2:
+                woven_z1[0] = make_z1(c, 0, gelus[0])
+            if not last and PRE[c] >= 3:
+                gelus[1] = gelu_rows(c, 1)
+            y_tiles = [weighted(second_stage(q, weights, acts, width), factor_sb) for q in range(early)]
             z1_q = []
             for q in range(4):
                 if q == early:
                     for b in range(2):
-                        z1_q.append(quantise("z1_%d%d" % (c, b), make_z1(c, b, gelu_rows(c, b)), CHUNKS[c][1]))
-                    y_tiles.append(second_stage(q, weights, acts, width, late=True))
-                nc.vector.tensor_tensor(page[q][:].indirect(where), y_tiles[q][:, 0:width], factor_sb, ALU.mult)
+                        if b not in gelus:
+                            gelus[b] = gelu_rows(c, b)
+                        if b not in woven_z1:
+                            woven_z1[b] = make_z1(c, b, gelus[b])
+                        z1_q.append(quantise("z1_%d%d" % (c, b), woven_z1[b], CHUNKS[c][1]))
+                    y_tiles.append(weighted(second_stage(q, weights, acts, width, GSLOT[2 * c + 1]), factor_sb))
+                if FUSED:
+                    nc.vector.tensor_tensor(page[q][:].indirect(where), y_tiles[q][:, 0:width], factor_sb, ALU.mult)
+                else:
+                    nc.vector.tensor_copy(page[q][:].indirect(where), y_tiles[q][:, 0:width])
                 if last:
                     nc.sync.dma_start(out=out[P * q : P * (q + 1), :], in_=page[q][:])
             acts = z1_q

import math
from contextlib import ExitStack

import concourse.mybir as mybir

K, M, H, N, T, S, PK, T2 = 1024, 512, 1024, 512, 2048, 1024, 512, 2048
FLOPS = 2 * (K * H * S + M * H * PK + H * N * S + H * N * PK)

F32 = mybir.dt.float32
BF16 = mybir.dt.bfloat16
I32 = mybir.dt.int32
U32 = mybir.dt.uint32
U16 = mybir.dt.uint16
U8 = mybir.dt.uint8
FP8X4 = mybir.dt.float8_e4m3fn_x4
FP4X4 = mybir.dt.float4_e2m1fn_x4
ACT = mybir.ActivationFunctionType
ALU = mybir.AluOpType

P = 128
W = 512
TWO_PI = 2.0 * math.pi

W1_ENGINE = ("scalar", "scalar", "vector", "vector")
W3_ENGINE = ("scalar", "scalar")
Z2_ENGINE = ("vector", "vector")
Z1_HOW = "VSSS"
WHOLE_ON_SCALAR = ()
PRE = (1, 2)
GSLOT = "JKGH"
FUSED = True
CHUNKS = ((0, 512), (512, 512))


def tile_list_repayment_feature_page_kernel(
    tc, tab_words, tab_scales, tab2_words, tab2_scales, offs, offs2, pos1, offs3, offs4, w1, w2_words, w2_scales,
    beta, phase, w3, w4_words, w4_scales, wg1, wg2, page1, out,
):
    nc = tc.nc
    with ExitStack() as ctx:
        lists = ctx.enter_context(tc.tile_pool(name="lists", bufs=1))
        keep = ctx.enter_context(tc.tile_pool(name="keep", bufs=1))
        slots = ctx.enter_context(tc.tile_pool(name="slots", bufs=1))
        ring = ctx.enter_context(tc.tile_pool(name="ring", bufs=4))
        psum = ctx.enter_context(tc.psum_pool(name="psum", bufs=8))

        def held(name, shape, dtype):
            return keep.tile(shape, dtype, name=name, align_bytes=64)

        def slot(tag, name, shape, dtype):
            return slots.tile(shape, dtype, name=name, tag=tag, align_bytes=64)

        def load_list(name, src):
            tl = lists.tile(list(src.shape), U16, name=name)
            nc.sync.dma_start(tl[:], src)
            return tl

        def zeroed_plane(name, width):
            plane = held(name, [P, width], U8)
            nc.vector.memset(plane[:].bitcast(I32), 0)
            return plane

        def load_plane(queue, plane, src):
            passes = src.shape[0]
            for q in range(4):
                queue.dma_start(out=plane[32 * q : 32 * q + 4 * passes, :].bitcast(I32),
                                in_=src[:, 4 * q : 4 * q + 4, :].bitcast(I32))

        def load_words(tl, src):
            nc.sync.dma_start(out=tl[:], in_=src.rearrange("p n i -> p (n i)").bitcast(I32))

        def load_rows(tl, src):
            nc.sync.dma_start(out=tl[:], in_=src.rearrange("(p i) c -> p i c", i=4))

        def bank():
            return psum.tile([P, W], F32, name="bank")

        def cast(engine, dst, src):
            if engine == "vector":
                nc.vector.tensor_copy(out=dst, in_=src)
            elif engine == "gpsimd":
                nc.gpsimd.tensor_scalar(out=dst, in0=src, scalar1=1.0, scalar2=0.0, op0=ALU.mult, op1=ALU.add)
            else:
                nc.scalar.copy(out=dst, in_=src)

        def quantise(name, grouped, width=W):
            codes = held(name + "_codes", [P, width], U32)
            scales = held(name + "_scales", [P, width], U8)
            nc.vector.quantize_mx(out=codes[:].bitcast(FP8X4), scales=scales[:], in_=grouped[:])
            return codes, scales

        def staged(width=W):
            return ring.tile([P, 4 * width], BF16, name="grouped", align_bytes=64)

        def woven(tl):
            return tl[:].rearrange("p (c e t) -> p c t e", e=4, t=4)

        def by_rows(tl):
            return tl[:].rearrange("p t (c e) -> p c t e", e=4)

        tab_plane = zeroed_plane("tab_plane", T)
        w2_plane = zeroed_plane("w2_plane", H)
        tab2_plane = zeroed_plane("tab2_plane", T)
        w4_plane = zeroed_plane("w4_plane", N)

        w1_raw = {}

        def load_w1(a, b, tag):
            w1_raw[a, b] = slot(tag, "w1_raw%d%d" % (a, b), [P, 4, W], F32)
            load_rows(w1_raw[a, b], w1[W * a : W * (a + 1), W * b : W * (b + 1)])

        w2_raw = held("w2_raw", [P, H // 2], I32)
        tab2_sb = slot("A", "tab2_sb", [P, T], I32)
        phase_sb = held("phase_sb", [P, 2, 4], F32)
        tab_sb = [slot("D", "tab_sb0", [P, T], I32), slot("E", "tab_sb1", [P, T], I32)]
        nc.sync.dma_start(out=w2_raw[:], in_=w2_words[0].bitcast(I32))
        idx = load_list("idx", offs)
        load_plane(nc.sync, tab_plane, tab_scales)
        idx2 = load_list("idx2", offs2)
        load_words(tab2_sb, tab2_words[0])
        load_w1(0, 0, "B")
        load_plane(nc.sync, w2_plane, w2_scales)
        load_plane(nc.sync, tab2_plane, tab2_scales)
        nc.sync.dma_start(out=phase_sb[:], in_=phase.rearrange("(b p t) -> p b t", p=P, t=4))
        load_words(tab_sb[0], tab_words[0])
        load_w1(1, 0, "C")
        load_words(tab_sb[1], tab_words[1])
        load_w1(0, 1, "F")
        load_w1(1, 1, "G")
        idx_p = load_list("idx_p", pos1)
        beta_sb = held("beta_sb", [P, 2, 4], F32)
        nc.sync.dma_start(out=beta_sb[:], in_=beta.rearrange("(b p t) -> p b t", p=P, t=4))

        w1_q = {}

        def round_w1(a, b):
            grouped = staged()
            cast(W1_ENGINE[2 * b + a], grouped[:].rearrange("p (t m i) -> p m i t", t=4, i=4),
                 w1_raw[a, b][:].rearrange("p i (m t) -> p m i t", t=4))
            return grouped

        def quantise_w1(a, b, grouped):
            w1_q[a, b] = quantise("w1_%d%d" % (a, b), grouped)

        v_codes = [held("v_codes0", [P, S], U32), held("v_codes1", [P, S], U32)]
        v_scales = held("v_scales", [P, S], U8)
        nc.vector.tensor_copy(v_scales[:], tab_plane[:].indirect(idx[:]))
        w2_dealt = held("w2_dealt", [P, H], U16)
        nc.vector.tensor_copy(out=w2_dealt[:].rearrange("p (b t m) -> p b m t", b=2, t=4),
                              in_=w2_raw[:].bitcast(U16).rearrange("p (b m t) -> p b m t", b=2, t=4))
        v2_codes = held("v2_codes", [P, PK], U32)
        nc.vector.tensor_copy(v2_codes[:], tab2_sb[:].bitcast(U32).indirect(idx2[:]))
        w2_plane_dealt = held("w2_plane_dealt", [P, H], U8)
        nc.vector.tensor_copy(out=w2_plane_dealt[:].rearrange("p (b t m) -> p b m t", b=2, t=4),
                              in_=w2_plane[:].rearrange("p (b m t) -> p b m t", b=2, t=4))
        v2_scales = held("v2_scales", [P, PK], U8)
        nc.vector.tensor_copy(v2_scales[:], tab2_plane[:].indirect(idx2[:]))
        turns0 = held("turns0", [P, 8], F32)
        nc.vector.tensor_scalar(out=turns0[:], in0=phase_sb[:].rearrange("p b t -> p (b t)"), scalar1=1.0 / TWO_PI,
                                scalar2=None, op0=ALU.mult)

        h1 = {}
        picked = [None, None]

        def first_stage(b):
            for t in range(4):
                h1[b, t] = held("h1_%d%d" % (b, t), [P, S], F32)
                for jh in range(2):
                    cols = slice(W * jh, W * (jh + 1))
                    acc = bank()
                    for a in range(2):
                        codes, scales = w1_q[a, b]
                        nc.tensor.matmul_mx(out=acc[:], lhsT=codes[:, P * t : P * (t + 1)].bitcast(FP8X4),
                                            lhsT_scale=scales[:, P * t : P * (t + 1)],
                                            rhs=v_codes[a][:, cols].bitcast(FP8X4), rhs_scale=v_scales[4 * a : P, cols],
                                            start=(a == 0), stop=(a == 1))
                    nc.scalar.copy(out=h1[b, t][:, cols], in_=acc[:])

        def pick(b):
            picked[b] = slot("CD"[b], "picked%d" % b, [P, 4, PK], F32)
            for t in range(4):
                nc.vector.tensor_tensor(picked[b][:, t, :], h1[b, t][:].indirect(idx_p[:]), turns[b][:, t, :], ALU.mult)

        turns = [slot("H", "turns_b0", [P, 4, PK], F32), slot("I", "turns_b1", [P, 4, PK], F32)]
        whole = [slot("J", "whole_b0", [P, 4, PK], I32), slot("K", "whole_b1", [P, 4, PK], I32)]

        def angles(b):
            for t in range(4):
                s = 4 * b + t
                acc = bank()
                nc.tensor.matmul_mx(out=acc[:], lhsT=w2_dealt[:, P * s : P * (s + 1)].bitcast(FP4X4),
                                    lhsT_scale=w2_plane_dealt[:, P * s : P * (s + 1)],
                                    rhs=v2_codes[:].bitcast(FP8X4), rhs_scale=v2_scales[:], start=True, stop=True)
                nc.scalar.activation(out=turns[b][:, t, :], in_=acc[:], func=ACT.Abs,
                                     bias=turns0[:, s : s + 1], scale=1.0 / TWO_PI)

        def reduce_turns(b):
            if b in WHOLE_ON_SCALAR:
                nc.scalar.activation(out=whole[b][:].bitcast(U32), in_=turns[b][:], func=ACT.Copy, bias=0.25, scale=1.0)
            else:
                nc.vector.tensor_scalar(out=whole[b][:], in0=turns[b][:], scalar1=0.25, scalar2=None, op0=ALU.add)
            nc.vector.scalar_tensor_tensor(out=turns[b][:], in0=turns[b][:], scalar=0.25, in1=whole[b][:],
                                           op0=ALU.add, op1=ALU.subtract)

        def cosine(b):
            nc.scalar.activation(out=turns[b][:], in_=turns[b][:], func=ACT.Sin, scale=TWO_PI)

        def make_z2(b):
            grouped = staged()
            cast(Z2_ENGINE[b], woven(grouped), by_rows(picked[b]))
            return grouped

        nc.vector.tensor_copy(v_codes[0][:], tab_sb[0][:].bitcast(U32).indirect(idx[:]))
        angles(0)
        w1_00 = round_w1(0, 0)
        nc.vector.tensor_copy(v_codes[1][:], tab_sb[1][:].bitcast(U32).indirect(idx[:]))
        w1_10 = round_w1(1, 0)
        quantise_w1(0, 0, w1_00)
        quantise_w1(1, 0, w1_10)
        angles(1)
        reduce_turns(0)
        cosine(0)
        first_stage(0)
        w1_01 = round_w1(0, 1)
        quantise_w1(0, 1, w1_01)
        w1_11 = round_w1(1, 1)
        quantise_w1(1, 1, w1_11)
        reduce_turns(1)
        pick(0)
        cosine(1)
        first_stage(1)
        w3_raw = [slot("A", "w3_raw0", [P, 4, W], F32), slot("B", "w3_raw1", [P, 4, W], F32)]
        w4_sb = held("w4_sb", [P, 2, N], I32)
        nc.sync.dma_start(out=w4_sb[:], in_=w4_words.rearrange("a p n i -> p a (n i)").bitcast(I32))
        load_plane(nc.sync, w4_plane, w4_scales)
        load_rows(w3_raw[0], w3[0:W, :])
        load_rows(w3_raw[1], w3[W : 2 * W, :])
        idx4 = load_list("idx4", offs4)
        idx3 = load_list("idx3", offs3)
        wg2_sb = held("wg2_sb", [P, PK], F32)
        nc.sync.dma_start(out=wg2_sb[:], in_=wg2)
        page = [held("page0", [P, T2], F32), held("page1", [P, T2], F32),
                slot("E", "page2", [P, T2], F32), slot("F", "page3", [P, T2], F32)]
        for q in range(4):
            nc.sync.dma_start(out=page[q][:], in_=page1[P * q : P * (q + 1), :])
        wg1_sb = held("wg1_sb", [P, S], F32)
        nc.sync.dma_start(out=wg1_sb[:], in_=wg1)

        inv_beta = held("inv_beta", [P, 8], F32)
        nc.vector.reciprocal(out=inv_beta[:], in_=beta_sb[:].rearrange("p b t -> p (b t)"))

        def second_stage(q, weights, acts, width, late=""):
            acc = bank()
            for b in range(2):
                w_codes, w_scales = weights[b]
                z_codes, z_scales = acts[b]
                nc.tensor.matmul_mx(out=acc[:, 0:width], lhsT=w_codes[:, P * q : P * (q + 1)].bitcast(FP8X4),
                                    lhsT_scale=w_scales[:, P * q : P * (q + 1)],
                                    rhs=z_codes[:, 0:width].bitcast(FP8X4), rhs_scale=z_scales[:, 0:width],
                                    start=(b == 0), stop=(b == 1))
            y = slot(late, "y_late", [P, W], F32) if late else keep.tile([P, W], F32, name="y", tag="y", bufs=4)
            nc.scalar.copy(out=y[:, 0:width], in_=acc[:, 0:width])
            return y

        def weighted(y, factor_sb):
            if not FUSED:
                nc.gpsimd.tensor_tensor(out=y[:], in0=y[:], in1=factor_sb, op=ALU.mult)
            return y

        def gelu_rows(c, b):
            j0, width = CHUNKS[c]
            g = slot(GSLOT[2 * c + b], "g%d%d" % (c, b), [P, 4, width], F32)
            for t in range(4):
                nc.scalar.activation(out=g[:, t, :], in_=h1[b, t][:, j0 : j0 + width], func=ACT.Gelu_apprx_tanh,
                                     scale=beta_sb[:, b, t : t + 1])
            return g

        def make_z1(c, b, g):
            width = CHUNKS[c][1]
            grouped = staged(width)
            how = Z1_HOW[2 * c + b]
            if how in "VG":
                factor = inv_beta[:, 4 * b : 4 * b + 4].unsqueeze(1).unsqueeze(3).to_broadcast([P, width // 4, 4, 4])
                engine = nc.vector if how == "V" else nc.gpsimd
                engine.tensor_tensor(out=woven(grouped), in0=by_rows(g), in1=factor, op=ALU.mult)
            else:
                rows = keep.tile([P, 4, width], BF16, name="z1_rows", tag="z1_rows", bufs=2)
                for t in range(4):
                    nc.scalar.activation(out=rows[:, t, :], in_=g[:, t, :], func=ACT.Copy,
                                         scale=inv_beta[:, 4 * b + t : 4 * b + t + 1])
                cast("scalar" if how == "S" else "gpsimd", woven(grouped), by_rows(rows))
            return grouped

        def round_w3(b):
            grouped = staged()
            cast(W3_ENGINE[b], woven(grouped), by_rows(w3_raw[b]))
            return grouped

        w4_q = [(w4_sb[:, b, :].bitcast(U32), w4_plane[4 * b : P, :]) for b in range(2)]
        z2_0 = make_z2(0)
        pick(1)
        w3_0 = round_w3(0)
        z2_q = [quantise("z2_0", z2_0)]
        z2_1 = make_z2(1)
        w3_q = [quantise("w3_0", w3_0)]
        z2_q.append(quantise("z2_1", z2_1))
        w3_1 = round_w3(1)
        w3_q.append(quantise("w3_1", w3_1))
        stages = [(w4_q, PK, idx4[:], wg2_sb[:])]
        stages.extend((w3_q, width, idx3[:, j0 // 16 : (j0 + width) // 16], wg1_sb[:, j0 : j0 + width]) for j0, width in CHUNKS)
        acts = z2_q
        for c, (weights, width, where, factor_sb) in enumerate(stages):
            last = c == len(CHUNKS)
            early = 4 if last else 3
            gelus, woven_z1 = {}, {}
            if not last and PRE[c] >= 1:
                gelus[0] = gelu_rows(c, 0)
            if not last and PRE[c] >= 2:
                woven_z1[0] = make_z1(c, 0, gelus[0])
            if not last and PRE[c] >= 3:
                gelus[1] = gelu_rows(c, 1)
            y_tiles = [weighted(second_stage(q, weights, acts, width), factor_sb) for q in range(early)]
            z1_q = []
            for q in range(4):
                if q == early:
                    for b in range(2):
                        if b not in gelus:
                            gelus[b] = gelu_rows(c, b)
                        if b not in woven_z1:
                            woven_z1[b] = make_z1(c, b, gelus[b])
                        z1_q.append(quantise("z1_%d%d" % (c, b), woven_z1[b], CHUNKS[c][1]))
                    y_tiles.append(weighted(second_stage(q, weights, acts, width, GSLOT[2 * c + 1]), factor_sb))
                if FUSED:
                    nc.vector.tensor_tensor(page[q][:].indirect(where), y_tiles[q][:, 0:width], factor_sb, ALU.mult)
                else:
                    nc.vector.tensor_copy(page[q][:].indirect(where), y_tiles[q][:, 0:width])
                if last:
                    nc.sync.dma_start(out=out[P * q : P * (q + 1), :], in_=page[q][:])
            acts = z1_q
